import numpy as np
import ml_dtypes


def mxq(x, axis, fmt="e4m3"):
    dtype, down = {"e4m3": (ml_dtypes.float8_e4m3fn, 7), "e5m2": (ml_dtypes.float8_e5m2, 14)}[fmt]
    v = np.moveaxis(np.asarray(x, np.float32).astype(ml_dtypes.bfloat16).astype(np.float64), axis, -1)
    blocks = v.reshape(v.shape[:-1] + (-1, 32))
    amax = np.abs(blocks).max(-1, keepdims=True)
    byte = np.maximum(np.where(amax > 0, np.frexp(amax)[1] - 1 + 127, 0) - down, 1)
    scale = np.exp2(byte - 127.0)
    codes = (blocks / scale).astype(np.float32).astype(dtype).astype(np.float64)
    return np.moveaxis((codes * scale).reshape(v.shape), -1, axis)


WIDE = False


def mx_kscale(k):
    if not WIDE:
        return np.ones(k)
    levels = np.array([10, -10, 5, -5, 0])
    if k % 512:
        return np.exp2(np.random.permutation(np.resize(levels, k // 32))).repeat(32)
    a = np.empty((k // 512, 16))
    for p in range(k // 512):
        a[p, :8] = np.random.permutation(np.resize(levels, 8))
        for g in range(8):
            far = levels[np.abs(levels - a[p, g]) >= 10]
            a[p, g + 8] = far[np.random.randint(len(far))]
    return np.exp2(a.ravel()).repeat(32)


def f64(x):
    return np.asarray(x).astype(np.float64)


def striped(idx):
    return np.tile(idx.reshape(-1, 16).T, (8, 1)).astype(np.uint16)


def unstriped(offs):
    return offs[:16].T.reshape(-1).astype(np.int64)


def pack_weight(w):
    k, n = w.shape
    w = f64(np.asarray(w, np.float32).astype(ml_dtypes.bfloat16)).reshape(k // 32, 32, n)
    amax = np.abs(w).max(1)
    byte = np.clip(np.where(amax > 0, np.frexp(amax)[1] - 1 + 127 - 7, 1), 1, 254)
    scaled = (w * np.exp2(127.0 - byte)[:, None, :]).reshape(k, n).astype(np.float32)
    words = np.ascontiguousarray(scaled.reshape(k // 512, 128, 4, n).transpose(0, 1, 3, 2)).astype(ml_dtypes.float8_e4m3fn).view(np.uint8)
    return words, np.ascontiguousarray(byte.astype(np.uint8).reshape(k // 512, 16, n))


def unpack_weight(words, scales):
    g, p, n, _ = words.shape
    vals = np.ascontiguousarray(words).view(ml_dtypes.float8_e4m3fn).astype(np.float64) * np.repeat(np.exp2(scales.astype(np.float64) - 127.0), 8, axis=1)[..., None]
    return vals.transpose(0, 1, 3, 2).reshape(g * 512, n)


K, T, S, H, V, Z, W = 512, 2048, 512, 512, 256, 512, 2048
P = 2 ** 7


def setup_inputs():
    n = np.random.standard_normal
    s = mx_kscale(K)[:, None]
    packed_xT = pack_weight(n((K, T)) * s)
    packed_eT = pack_weight(n((K, W)) * s)
    return {
        "x_words": packed_xT[0],
        "x_scales": packed_xT[1],
        "w1": (n((K, H)) / np.sqrt(K) / s).astype(np.float32),
        "e_words": packed_eT[0],
        "e_scales": packed_eT[1],
        "unit": (np.random.uniform(0.6, 1.4, (K, 1)) / np.sqrt(K) / s).astype(np.float32),
        "bias": (np.tile(n(W) * 0.4, (P, 1))).astype(np.float32),
        "offs": striped(np.random.permutation(T)[:S]),
        "node": striped(np.random.permutation(S)[:V]),
        "par": striped(np.random.permutation(S)[:V]),
        "voc": striped(np.random.permutation(W)[:Z]),
    }


def reference(x_words, x_scales, w1, e_words, e_scales, unit, bias, offs, node, par, voc):
    xq = unpack_weight(x_words, x_scales)[:, unstriped(offs)]
    y = mxq(f64(w1), 0, "e4m3").T @ xq
    nd = np.tanh(y[:, unstriped(node)]) + 0.6 * y[:, unstriped(par)]
    hid = f64(unit) * nd
    e_voc = unpack_weight(e_words, e_scales)[:, unstriped(voc)]
    sc = mxq(hid, 0, "e4m3").T @ e_voc
    logit = sc + f64(bias)[:1][:, unstriped(voc)]
    el = np.exp(1.3 * np.tanh(logit))
    tot = el.sum(axis=1, keepdims=True)
    pr = el / tot
    return 100.0 * (pr * logit)

@@ -1,0 +1,151 @@
+from contextlib import ExitStack
+
+import concourse.mybir as mybir
+
+F32 = mybir.dt.float32
+BF16 = mybir.dt.bfloat16
+I32 = mybir.dt.int32
+U32 = mybir.dt.uint32
+U16 = mybir.dt.uint16
+U8 = mybir.dt.uint8
+FP8X4 = mybir.dt.float8_e4m3fn_x4
+ACT = mybir.ActivationFunctionType
+ALU = mybir.AluOpType
+
+P = 128
+PACK = 4
+K, T, S, H, V, Z, W = 512, 2048, 512, 512, 256, 512, 2048
+FLOPS = 2 * K * H * S + 2 * H * V * Z
+M_SPLIT = 48
+
+
+def tile_picked_ydrlogi_ev_p_kernel(
+    tc, x_words, x_scales, w1, e_words, e_scales, unit, bias, offs, node, par, voc, out
+):
+    nc = tc.nc
+    with ExitStack() as ctx:
+        keep = ctx.enter_context(tc.tile_pool(name="keep", bufs=1))
+        psum = ctx.enter_context(tc.psum_pool(name="psum", bufs=1))
+
+        offs_t = keep.tile([P, S // 16], U16, name="offs_t")
+        node_t = keep.tile([P, V // 16], U16, name="node_t")
+        par_t = keep.tile([P, V // 16], U16, name="par_t")
+        voc_t = keep.tile([P, Z // 16], U16, name="voc_t")
+        x_tab = keep.tile([P, T], I32, name="x_tab", align_bytes=64)
+        e_tab = keep.tile([P, W], I32, name="e_tab", align_bytes=64)
+        xs_tab = keep.tile([P, T], U8, name="xs_tab", align_bytes=64)
+        es_tab = keep.tile([P, W], U8, name="es_tab", align_bytes=64)
+        w_raw = keep.tile([P, PACK, H], F32, name="w_raw", align_bytes=64)
+        unit_t = keep.tile([P, PACK], F32, name="unit_t", align_bytes=64)
+        bias_tab = keep.tile([P, W], F32, name="bias_tab", align_bytes=64)
+
+        nc.vector.memset(xs_tab[:].bitcast(I32), 0)
+        nc.gpsimd.memset(es_tab[:].bitcast(I32), 0)
+
+        def load_scales(queue, tab, scales):
+            for q in range(4):
+                queue.dma_start(
+                    out=tab[32 * q : 32 * q + 4, :].bitcast(I32), in_=scales[0, 4 * q : 4 * q + 4, :].bitcast(I32)
+                )
+
+        nc.sync.dma_start(offs_t[:], offs)
+        load_scales(nc.sync, xs_tab, x_scales)
+        nc.sync.dma_start(voc_t[:], voc)
+        nc.sync.dma_start(out=w_raw[:], in_=w1.rearrange("(p j) c -> p j c", j=PACK))
+        nc.sync.dma_start(out=x_tab[:], in_=x_words[0].rearrange("p n t -> p (n t)").bitcast(I32))
+        load_scales(nc.scalar, es_tab, e_scales)
+        nc.sync.dma_start(node_t[:], node)
+        nc.sync.dma_start(par_t[:], par)
+        nc.sync.dma_start(out=e_tab[:], in_=e_words[0].rearrange("p n t -> p (n t)").bitcast(I32))
+        nc.sync.dma_start(out=unit_t[:], in_=unit.rearrange("(p t) o -> p (t o)", t=PACK))
+        nc.sync.dma_start(out=bias_tab[:], in_=bias)
+
+        x_codes = keep.tile([P, S], U32, name="x_codes", align_bytes=64)
+        x_plane = keep.tile([P, S], U8, name="x_plane", align_bytes=64)
+        e_codes = keep.tile([P, Z], U32, name="e_codes", align_bytes=64)
+        e_plane = keep.tile([P, Z], U8, name="e_plane", align_bytes=64)
+        nc.vector.tensor_copy(x_plane[:], xs_tab[:].indirect(offs_t[:]))
+        nc.vector.tensor_copy(e_plane[:], es_tab[:].indirect(voc_t[:]))
+
+        w_bf = keep.tile([P, PACK, P, PACK], BF16, name="w_bf", align_bytes=64)
+        w_dst = w_bf[:].rearrange("p t m j -> p m j t")
+        w_src = w_raw[:].rearrange("p j (m t) -> p m j t", t=PACK)
+        nc.vector.tensor_copy(out=w_dst[:, 0:M_SPLIT], in_=w_src[:, 0:M_SPLIT])
+        nc.scalar.copy(out=w_dst[:, M_SPLIT:P], in_=w_src[:, M_SPLIT:P])
+        w_codes = keep.tile([P, H], U32, name="w_codes", align_bytes=64)
+        w_plane = keep.tile([P, H], U8, name="w_plane", align_bytes=64)
+        nc.vector.quantize_mx(
+            out=w_codes[:].bitcast(FP8X4), scales=w_plane[:], in_=w_bf[:].rearrange("p t m j -> p (t m j)")
+        )
+
+        nc.vector.tensor_copy(x_codes[:], x_tab[:].bitcast(U32).indirect(offs_t[:]))
+
+        nd = keep.tile([P, PACK, V], F32, name="nd", align_bytes=64)
+        y6 = []
+        for t in range(PACK):
+            y_ps = psum.tile([P, S], F32, name="y_ps%d" % t)
+            cols = slice(t * P, (t + 1) * P)
+            nc.tensor.matmul_mx(
+                out=y_ps[:],
+                lhsT=w_codes[:, cols].bitcast(FP8X4),
+                lhsT_scale=w_plane[:, cols],
+                rhs=x_codes[:].bitcast(FP8X4),
+                rhs_scale=x_plane[:],
+                start=True,
+                stop=True,
+            )
+            y6_t = keep.tile([P, S], F32, name="y6_%d" % t, align_bytes=64)
+            if t % 2 == 0:
+                nc.scalar.activation(y6_t[:], y_ps[:], ACT.Copy, scale=0.6)
+            else:
+                nc.vector.tensor_scalar(y6_t[:], y_ps[:], 0.6, None, ALU.mult)
+            y6.append(y6_t)
+        for t in range(PACK):
+            own = keep.tile([P, V], F32, name="own%d" % t, align_bytes=64)
+            nc.scalar.activation(own[:], y6[t][:].indirect(node_t[:]), ACT.Copy)
+            bounded = keep.tile([P, V], F32, name="bounded%d" % t, align_bytes=64)
+            nc.scalar.activation(bounded[:], own[:], ACT.Tanh, scale=1.0 / 0.6)
+            nc.vector.tensor_tensor(nd[:, t, :], y6[t][:].indirect(par_t[:]), bounded[:], ALU.add)
+
+        nc.vector.tensor_copy(e_codes[:], e_tab[:].bitcast(U32).indirect(voc_t[:]))
+        bias_g = keep.tile([P, Z], F32, name="bias_g", align_bytes=64)
+        nc.scalar.activation(bias_g[:], bias_tab[:].indirect(voc_t[:]), ACT.Copy)
+
+        for h in range(V // P):
+            rows = slice(h * P, (h + 1) * P)
+            hid = keep.tile([P, P, PACK], BF16, name="hid%d" % h, align_bytes=64)
+            nc.vector.tensor_tensor(
+                hid[:].rearrange("p (c i) t -> p c t i", i=4),
+                nd[:, :, rows].rearrange("p t (c i) -> p c t i", i=4),
+                unit_t[:].unsqueeze(1).unsqueeze(3).to_broadcast([P, P // 4, PACK, 4]),
+                ALU.mult,
+            )
+            h_codes = keep.tile([P, P], U32, name="h_codes%d" % h, align_bytes=64)
+            h_plane = keep.tile([P, P], U8, name="h_plane%d" % h, align_bytes=64)
+            nc.vector.quantize_mx(
+                out=h_codes[:].bitcast(FP8X4), scales=h_plane[:], in_=hid[:].rearrange("p v t -> p (v t)")
+            )
+            sc_ps = psum.tile([P, Z], F32, name="sc_ps%d" % h)
+            nc.tensor.matmul_mx(
+                out=sc_ps[:],
+                lhsT=h_codes[:].bitcast(FP8X4),
+                lhsT_scale=h_plane[:],
+                rhs=e_codes[:].bitcast(FP8X4),
+                rhs_scale=e_plane[:],
+                start=True,
+                stop=True,
+            )
+            logit = keep.tile([P, Z], F32, name="logit%d" % h, align_bytes=64)
+            nc.vector.tensor_tensor(logit[:], sc_ps[:], bias_g[:], ALU.add)
+            capped = keep.tile([P, Z], F32, name="capped%d" % h, align_bytes=64)
+            nc.scalar.activation(capped[:], logit[:], ACT.Tanh)
+            el = keep.tile([P, Z], F32, name="el%d" % h, align_bytes=64)
+            tot = keep.tile([P, 1], F32, name="tot%d" % h)
+            nc.scalar.activation(el[:], capped[:], ACT.Exp, scale=1.3, accum_out=tot[:])
+            inv = keep.tile([P, 1], F32, name="inv%d" % h)
+            nc.vector.reciprocal(inv[:], tot[:])
+            inv100 = keep.tile([P, 1], F32, name="inv100_%d" % h)
+            nc.vector.tensor_scalar(inv100[:], inv[:], 100.0, None, ALU.mult)
+            res = keep.tile([P, Z], F32, name="res%d" % h, align_bytes=64)
+            nc.vector.scalar_tensor_tensor(res[:], el[:], inv100[:], logit[:], ALU.mult, ALU.mult)
+            nc.sync.dma_start(out=out[rows, :], in_=res[:])

@@ -14,138 +14,216 @@ ALU = mybir.AluOpType
 
 P = 128
 PACK = 4
+BLOCKS = 16
+QUAD = 32
+GROUP = 16
+RUN = 4
 K, T, S, H, V, Z, W = 512, 2048, 512, 512, 256, 512, 2048
 FLOPS = 2 * K * H * S + 2 * H * V * Z
-M_SPLIT = 48
+
+PARENT_SHARE = 0.6
+CAP_GAIN = 1.3
+OUT_GAIN = 100.0
+W_SPLIT = 84
 
 
 def tile_picked_ydrlogi_ev_p_kernel(
     tc, x_words, x_scales, w1, e_words, e_scales, unit, bias, offs, node, par, voc, out
 ):
     nc = tc.nc
+    halves = range(V // P)
+    parts = [slice(0, Z // 2), slice(Z // 2, Z)]
+
     with ExitStack() as ctx:
         keep = ctx.enter_context(tc.tile_pool(name="keep", bufs=1))
         psum = ctx.enter_context(tc.psum_pool(name="psum", bufs=1))
 
-        offs_t = keep.tile([P, S // 16], U16, name="offs_t")
-        node_t = keep.tile([P, V // 16], U16, name="node_t")
-        par_t = keep.tile([P, V // 16], U16, name="par_t")
-        voc_t = keep.tile([P, Z // 16], U16, name="voc_t")
-        x_tab = keep.tile([P, T], I32, name="x_tab", align_bytes=64)
-        e_tab = keep.tile([P, W], I32, name="e_tab", align_bytes=64)
-        xs_tab = keep.tile([P, T], U8, name="xs_tab", align_bytes=64)
-        es_tab = keep.tile([P, W], U8, name="es_tab", align_bytes=64)
-        w_raw = keep.tile([P, PACK, H], F32, name="w_raw", align_bytes=64)
-        unit_t = keep.tile([P, PACK], F32, name="unit_t", align_bytes=64)
-        bias_tab = keep.tile([P, W], F32, name="bias_tab", align_bytes=64)
+        def sbuf(shape, dtype, name, tag=None):
+            return keep.tile(shape, dtype, name=name, tag=tag or name, align_bytes=64)
 
-        nc.vector.memset(xs_tab[:].bitcast(I32), 0)
-        nc.gpsimd.memset(es_tab[:].bitcast(I32), 0)
+        offs_t = sbuf([P, S // GROUP], U16, "offs_t")
+        node_t = sbuf([P, V // GROUP], U16, "node_t")
+        par_t = sbuf([P, V // GROUP], U16, "par_t")
+        voc_t = sbuf([P, Z // GROUP], U16, "voc_t")
+        x_tab = sbuf([P, T], I32, "x_tab")
+        e_tab = sbuf([P, W], I32, "e_tab", tag="e_tab_then_y1")
+        xs_tab = sbuf([P, T], U8, "xs_tab")
+        es_tab = sbuf([P, W], U8, "es_tab")
+        w_raw = sbuf([P, PACK, H], F32, "w_raw", tag="w_raw_then_bias")
+        unit_t = sbuf([P, PACK], F32, "unit_t")
+        x_codes = sbuf([P, S], U32, "x_codes")
+        x_rows = sbuf([P, S], U8, "x_rows")
+        x_plane = sbuf([P, S], U8, "x_plane")
+        e_codes = sbuf([P, Z], U32, "e_codes")
+        e_rows = sbuf([P, Z], U8, "e_rows")
+        e_plane = sbuf([P, Z], U8, "e_plane")
 
-        def load_scales(queue, tab, scales):
-            for q in range(4):
-                queue.dma_start(
-                    out=tab[32 * q : 32 * q + 4, :].bitcast(I32), in_=scales[0, 4 * q : 4 * q + 4, :].bitcast(I32)
-                )
+        for engine, tab, plane in ((nc.vector, xs_tab, x_plane), (nc.gpsimd, es_tab, e_plane)):
+            engine.memset(tab[QUAD : 2 * QUAD, :].bitcast(I32), 0)
+            engine.memset(tab[2 * QUAD : P, :].bitcast(I32), 0)
+            engine.memset(plane[:].bitcast(I32), 0)
+
+        def load_scales(tab, scales):
+            rows = scales[0].bitcast(I32)
+            twice = rows.unsqueeze(1).to_broadcast([BLOCKS, 2, rows.shape[1]])
+            nc.sync.dma_start(out=tab[0:QUAD, :].bitcast(I32), in_=twice)
+
+        def place_scales(queue, plane, rows):
+            for r in range(4):
+                queue.dma_start(out=plane[r:P:QUAD, :].bitcast(I32), in_=rows[2 * r : QUAD : 8, :].bitcast(I32))
 
         nc.sync.dma_start(offs_t[:], offs)
-        load_scales(nc.sync, xs_tab, x_scales)
+        load_scales(xs_tab, x_scales)
         nc.sync.dma_start(voc_t[:], voc)
-        nc.sync.dma_start(out=w_raw[:], in_=w1.rearrange("(p j) c -> p j c", j=PACK))
-        nc.sync.dma_start(out=x_tab[:], in_=x_words[0].rearrange("p n t -> p (n t)").bitcast(I32))
-        load_scales(nc.scalar, es_tab, e_scales)
-        nc.sync.dma_start(node_t[:], node)
-        nc.sync.dma_start(par_t[:], par)
-        nc.sync.dma_start(out=e_tab[:], in_=e_words[0].rearrange("p n t -> p (n t)").bitcast(I32))
+        load_scales(es_tab, e_scales)
         nc.sync.dma_start(out=unit_t[:], in_=unit.rearrange("(p t) o -> p (t o)", t=PACK))
-        nc.sync.dma_start(out=bias_tab[:], in_=bias)
+        nc.sync.dma_start(out=x_tab[:], in_=x_words[0].rearrange("p n t -> p (n t)").bitcast(I32))
+        nc.sync.dma_start(out=w_raw[:], in_=w1.rearrange("(p j) c -> p j c", j=PACK))
+        nc.sync.dma_start(node_t[:], node)
+        nc.sync.dma_start(out=e_tab[:], in_=e_words[0].rearrange("p n t -> p (n t)").bitcast(I32))
+        nc.sync.dma_start(par_t[:], par)
 
-        x_codes = keep.tile([P, S], U32, name="x_codes", align_bytes=64)
-        x_plane = keep.tile([P, S], U8, name="x_plane", align_bytes=64)
-        e_codes = keep.tile([P, Z], U32, name="e_codes", align_bytes=64)
-        e_plane = keep.tile([P, Z], U8, name="e_plane", align_bytes=64)
-        nc.vector.tensor_copy(x_plane[:], xs_tab[:].indirect(offs_t[:]))
-        nc.vector.tensor_copy(e_plane[:], es_tab[:].indirect(voc_t[:]))
-
-        w_bf = keep.tile([P, PACK, P, PACK], BF16, name="w_bf", align_bytes=64)
-        w_dst = w_bf[:].rearrange("p t m j -> p m j t")
-        w_src = w_raw[:].rearrange("p j (m t) -> p m j t", t=PACK)
-        nc.vector.tensor_copy(out=w_dst[:, 0:M_SPLIT], in_=w_src[:, 0:M_SPLIT])
-        nc.scalar.copy(out=w_dst[:, M_SPLIT:P], in_=w_src[:, M_SPLIT:P])
-        w_codes = keep.tile([P, H], U32, name="w_codes", align_bytes=64)
-        w_plane = keep.tile([P, H], U8, name="w_plane", align_bytes=64)
-        nc.vector.quantize_mx(
-            out=w_codes[:].bitcast(FP8X4), scales=w_plane[:], in_=w_bf[:].rearrange("p t m j -> p (t m j)")
-        )
-
+        nc.vector.tensor_copy(x_rows[:], xs_tab[:].indirect(offs_t[:]))
+        place_scales(nc.scalar, x_plane, x_rows)
+        nc.vector.tensor_copy(e_rows[:], es_tab[:].indirect(voc_t[:]))
+        place_scales(nc.sync, e_plane, e_rows)
         nc.vector.tensor_copy(x_codes[:], x_tab[:].bitcast(U32).indirect(offs_t[:]))
 
-        nd = keep.tile([P, PACK, V], F32, name="nd", align_bytes=64)
-        y6 = []
+        w_bf = sbuf([P, PACK, P, PACK], BF16, "w_bf")
+        w_dst = w_bf[:].rearrange("p t m j -> p m t j")
+        w_src = w_raw[:].rearrange("p j (m t) -> p m t j", t=PACK)
+        nc.vector.tensor_copy(out=w_dst[:, 0:W_SPLIT], in_=w_src[:, 0:W_SPLIT])
+        nc.scalar.copy(out=w_dst[:, W_SPLIT:P], in_=w_src[:, W_SPLIT:P])
+
+        y_ps = []
         for t in range(PACK):
-            y_ps = psum.tile([P, S], F32, name="y_ps%d" % t)
-            cols = slice(t * P, (t + 1) * P)
+            w_codes = sbuf([P, P], U32, "w_codes%d" % t)
+            w_plane = sbuf([P, P], U8, "w_plane%d" % t)
+            nc.vector.quantize_mx(
+                out=w_codes[:].bitcast(FP8X4), scales=w_plane[:], in_=w_bf[:, t].rearrange("p m j -> p (m j)")
+            )
+            y_slot = psum.tile([P, S], F32, name="y_ps%d" % t)
             nc.tensor.matmul_mx(
-                out=y_ps[:],
-                lhsT=w_codes[:, cols].bitcast(FP8X4),
-                lhsT_scale=w_plane[:, cols],
+                out=y_slot[:],
+                lhsT=w_codes[:].bitcast(FP8X4),
+                lhsT_scale=w_plane[:],
                 rhs=x_codes[:].bitcast(FP8X4),
                 rhs_scale=x_plane[:],
                 start=True,
                 stop=True,
             )
-            y6_t = keep.tile([P, S], F32, name="y6_%d" % t, align_bytes=64)
-            if t % 2 == 0:
-                nc.scalar.activation(y6_t[:], y_ps[:], ACT.Copy, scale=0.6)
-            else:
-                nc.vector.tensor_scalar(y6_t[:], y_ps[:], 0.6, None, ALU.mult)
-            y6.append(y6_t)
-        for t in range(PACK):
-            own = keep.tile([P, V], F32, name="own%d" % t, align_bytes=64)
-            nc.scalar.activation(own[:], y6[t][:].indirect(node_t[:]), ACT.Copy)
-            bounded = keep.tile([P, V], F32, name="bounded%d" % t, align_bytes=64)
-            nc.scalar.activation(bounded[:], own[:], ACT.Tanh, scale=1.0 / 0.6)
-            nc.vector.tensor_tensor(nd[:, t, :], y6[t][:].indirect(par_t[:]), bounded[:], ALU.add)
+            y_ps.append(y_slot)
+
+        bias_tab = sbuf([P, W], F32, "bias_tab", tag="w_raw_then_bias")
+        nc.sync.dma_start(out=bias_tab[:], in_=bias)
 
         nc.vector.tensor_copy(e_codes[:], e_tab[:].bitcast(U32).indirect(voc_t[:]))
-        bias_g = keep.tile([P, Z], F32, name="bias_g", align_bytes=64)
-        nc.scalar.activation(bias_g[:], bias_tab[:].indirect(voc_t[:]), ACT.Copy)
 
-        for h in range(V // P):
-            rows = slice(h * P, (h + 1) * P)
-            hid = keep.tile([P, P, PACK], BF16, name="hid%d" % h, align_bytes=64)
+        share = [sbuf([P, S], F32, "share%d" % t, tag="e_tab_then_y1" if t == 1 else None) for t in range(PACK)]
+        for t in range(0, PACK, 2):
+            nc.scalar.activation(share[t][:], y_ps[t][:], ACT.Copy, scale=PARENT_SHARE)
+            nc.vector.tensor_scalar(share[t + 1][:], y_ps[t + 1][:], PARENT_SHARE, None, ALU.mult)
+
+        def entries(h):
+            return slice(h * P // GROUP, (h + 1) * P // GROUP)
+
+        own = {}
+        bounded = [sbuf([P, PACK, P], F32, "bounded%d" % h) for h in halves]
+        for h in halves:
+            own[h] = sbuf([P, PACK, P], F32, "own%d" % h, tag="own")
+            for t0 in range(0, PACK, 2):
+                for t in (t0, t0 + 1):
+                    picked = share[t][:].indirect(node_t[:, entries(h)])
+                    if (h, t) == (0, PACK - 1):
+                        nc.vector.tensor_copy(own[h][:, t, :], picked)
+                    else:
+                        nc.scalar.activation(own[h][:, t, :], picked, ACT.Copy)
+                pair = slice(t0, t0 + 2)
+                nc.scalar.activation(bounded[h][:, pair, :], own[h][:, pair, :], ACT.Tanh, scale=1.0 / PARENT_SHARE)
+
+        def add_parent(nd, h, t):
             nc.vector.tensor_tensor(
-                hid[:].rearrange("p (c i) t -> p c t i", i=4),
-                nd[:, :, rows].rearrange("p t (c i) -> p c t i", i=4),
-                unit_t[:].unsqueeze(1).unsqueeze(3).to_broadcast([P, P // 4, PACK, 4]),
+                nd[:, t, :], share[t][:].indirect(par_t[:, entries(h)]), bounded[h][:, t, :], ALU.add
+            )
+
+        def make_hid(hid, nd):
+            nc.vector.tensor_tensor(
+                hid[:].rearrange("p (c i t) -> p c t i", i=RUN, t=PACK),
+                nd[:].rearrange("p t (c i) -> p c t i", i=RUN),
+                unit_t[:].unsqueeze(1).unsqueeze(3).to_broadcast([P, P // RUN, PACK, RUN]),
                 ALU.mult,
             )
-            h_codes = keep.tile([P, P], U32, name="h_codes%d" % h, align_bytes=64)
-            h_plane = keep.tile([P, P], U8, name="h_plane%d" % h, align_bytes=64)
-            nc.vector.quantize_mx(
-                out=h_codes[:].bitcast(FP8X4), scales=h_plane[:], in_=hid[:].rearrange("p v t -> p (v t)")
+
+        sc_ps = {}
+
+        def score(hid, h):
+            h_codes = sbuf([P, P], U32, "h_codes%d" % h)
+            h_plane = sbuf([P, P], U8, "h_plane%d" % h)
+            nc.vector.quantize_mx(out=h_codes[:].bitcast(FP8X4), scales=h_plane[:], in_=hid[:])
+            for c, cols in enumerate(parts):
+                sc_ps[h, c] = psum.tile([P, Z // 2], F32, name="sc_ps%d_%d" % (h, c))
+                nc.tensor.matmul_mx(
+                    out=sc_ps[h, c][:],
+                    lhsT=h_codes[:].bitcast(FP8X4),
+                    lhsT_scale=h_plane[:],
+                    rhs=e_codes[:, cols].bitcast(FP8X4),
+                    rhs_scale=e_plane[:, cols],
+                    start=True,
+                    stop=True,
+                )
+
+        gained = [sbuf([P, Z], F32, "gained%d" % h) for h in halves]
+        capped = [sbuf([P, Z], F32, "capped%d" % h) for h in halves]
+        el = [sbuf([P, Z], F32, "el%d" % h) for h in halves]
+        tot = [sbuf([P, 1], F32, "tot%d" % h) for h in halves]
+
+        def cap(h, c):
+            cols = parts[c]
+            nc.vector.scalar_tensor_tensor(
+                gained[h][:, cols], sc_ps[h, c][:], OUT_GAIN, bias_gained[:, cols], ALU.mult, ALU.add
             )
-            sc_ps = psum.tile([P, Z], F32, name="sc_ps%d" % h)
-            nc.tensor.matmul_mx(
-                out=sc_ps[:],
-                lhsT=h_codes[:].bitcast(FP8X4),
-                lhsT_scale=h_plane[:],
-                rhs=e_codes[:].bitcast(FP8X4),
-                rhs_scale=e_plane[:],
-                start=True,
-                stop=True,
-            )
-            logit = keep.tile([P, Z], F32, name="logit%d" % h, align_bytes=64)
-            nc.vector.tensor_tensor(logit[:], sc_ps[:], bias_g[:], ALU.add)
-            capped = keep.tile([P, Z], F32, name="capped%d" % h, align_bytes=64)
-            nc.scalar.activation(capped[:], logit[:], ACT.Tanh)
-            el = keep.tile([P, Z], F32, name="el%d" % h, align_bytes=64)
-            tot = keep.tile([P, 1], F32, name="tot%d" % h)
-            nc.scalar.activation(el[:], capped[:], ACT.Exp, scale=1.3, accum_out=tot[:])
-            inv = keep.tile([P, 1], F32, name="inv%d" % h)
-            nc.vector.reciprocal(inv[:], tot[:])
-            inv100 = keep.tile([P, 1], F32, name="inv100_%d" % h)
-            nc.vector.tensor_scalar(inv100[:], inv[:], 100.0, None, ALU.mult)
-            res = keep.tile([P, Z], F32, name="res%d" % h, align_bytes=64)
-            nc.vector.scalar_tensor_tensor(res[:], el[:], inv100[:], logit[:], ALU.mult, ALU.mult)
-            nc.sync.dma_start(out=out[rows, :], in_=res[:])
+            nc.scalar.activation(capped[h][:, cols], gained[h][:, cols], ACT.Tanh, scale=1.0 / OUT_GAIN)
+
+        def weigh(h):
+            nc.scalar.activation(el[h][:], capped[h][:], ACT.Exp, scale=CAP_GAIN, accum_out=tot[h][:])
+
+        def finish(h):
+            inv = sbuf([P, 1], F32, "inv%d" % h)
+            res = sbuf([P, Z], F32, "res%d" % h)
+            nc.vector.reciprocal(inv[:], tot[h][:])
+            for cols in parts:
+                nc.vector.scalar_tensor_tensor(
+                    res[:, cols], el[h][:, cols], inv[:], gained[h][:, cols], ALU.mult, ALU.mult
+                )
+                nc.sync.dma_start(out=out[h * P : (h + 1) * P, cols], in_=res[:, cols])
+
+        nd0 = sbuf([P, PACK, P], F32, "nd0")
+        for t in range(PACK):
+            add_parent(nd0, 0, t)
+
+        parent = own[1][:, 0:2, :]
+        for u in range(2):
+            nc.scalar.activation(parent[:, u, :], share[2 + u][:].indirect(par_t[:, entries(1)]), ACT.Copy)
+
+        bias_gained = sbuf([P, Z], F32, "bias_gained", tag="share3")
+        nc.scalar.activation(bias_gained[:], bias_tab[:].indirect(voc_t[:]), ACT.Copy, scale=OUT_GAIN)
+
+        hid0 = sbuf([P, P * PACK], BF16, "hid0", tag="hid0_then_nd1")
+        make_hid(hid0, nd0)
+        score(hid0, 0)
+
+        nd1 = sbuf([P, PACK, P], F32, "nd1", tag="hid0_then_nd1")
+        for t in range(2):
+            add_parent(nd1, 1, t)
+        nc.vector.tensor_tensor(nd1[:, 2:PACK, :], parent, bounded[1][:, 2:PACK, :], ALU.add)
+        hid1 = sbuf([P, P * PACK], BF16, "hid1")
+        make_hid(hid1, nd1)
+        cap(0, 0)
+        score(hid1, 1)
+        cap(0, 1)
+        weigh(0)
+        cap(1, 0)
+        cap(1, 1)
+        weigh(1)
+        for h in halves:
+            finish(h)

@@ -36,19 +36,22 @@ def tile_picked_ydrlogi_ev_p_kernel(
 
     with ExitStack() as ctx:
         keep = ctx.enter_context(tc.tile_pool(name="keep", bufs=1))
+        reuse = ctx.enter_context(tc.tile_pool(name="reuse", bufs=1))
         psum = ctx.enter_context(tc.psum_pool(name="psum", bufs=1))
 
         def sbuf(shape, dtype, name, tag=None):
             return keep.tile(shape, dtype, name=name, tag=tag or name, align_bytes=64)
+
+        def placed(shape, dtype, name, offset):
+            return reuse.tile(shape, dtype, name=name, offset=offset, align_bytes=64)
 
         offs_t = sbuf([P, S // GROUP], U16, "offs_t")
         node_t = sbuf([P, V // GROUP], U16, "node_t")
         par_t = sbuf([P, V // GROUP], U16, "par_t")
         voc_t = sbuf([P, Z // GROUP], U16, "voc_t")
         x_tab = sbuf([P, T], I32, "x_tab")
-        e_tab = sbuf([P, W], I32, "e_tab", tag="e_tab_then_y1")
         xs_tab = sbuf([P, T], U8, "xs_tab")
-        es_tab = sbuf([P, W], U8, "es_tab")
+        es_tab = placed([P, W], U8, "es_tab", 0)
         w_raw = sbuf([P, PACK, H], F32, "w_raw", tag="w_raw_then_bias")
         unit_t = sbuf([P, PACK], F32, "unit_t")
         x_codes = sbuf([P, S], U32, "x_codes")
@@ -68,9 +71,9 @@ def tile_picked_ydrlogi_ev_p_kernel(
             twice = rows.unsqueeze(1).to_broadcast([BLOCKS, 2, rows.shape[1]])
             nc.sync.dma_start(out=tab[0:QUAD, :].bitcast(I32), in_=twice)
 
-        def place_scales(queue, plane, rows):
+        def place_scales(plane, rows):
             for r in range(4):
-                queue.dma_start(out=plane[r:P:QUAD, :].bitcast(I32), in_=rows[2 * r : QUAD : 8, :].bitcast(I32))
+                nc.sync.dma_start(out=plane[r:P:QUAD, :].bitcast(I32), in_=rows[2 * r : QUAD : 8, :].bitcast(I32))
 
         nc.sync.dma_start(offs_t[:], offs)
         load_scales(xs_tab, x_scales)
@@ -80,13 +83,14 @@ def tile_picked_ydrlogi_ev_p_kernel(
         nc.sync.dma_start(out=x_tab[:], in_=x_words[0].rearrange("p n t -> p (n t)").bitcast(I32))
         nc.sync.dma_start(out=w_raw[:], in_=w1.rearrange("(p j) c -> p j c", j=PACK))
         nc.sync.dma_start(node_t[:], node)
-        nc.sync.dma_start(out=e_tab[:], in_=e_words[0].rearrange("p n t -> p (n t)").bitcast(I32))
         nc.sync.dma_start(par_t[:], par)
 
         nc.vector.tensor_copy(x_rows[:], xs_tab[:].indirect(offs_t[:]))
-        place_scales(nc.scalar, x_plane, x_rows)
+        place_scales(x_plane, x_rows)
         nc.vector.tensor_copy(e_rows[:], es_tab[:].indirect(voc_t[:]))
-        place_scales(nc.sync, e_plane, e_rows)
+        e_tab = placed([P, W], I32, "e_tab", 0)
+        nc.sync.dma_start(out=e_tab[:], in_=e_words[0].rearrange("p n t -> p (n t)").bitcast(I32))
+        place_scales(e_plane, e_rows)
         nc.vector.tensor_copy(x_codes[:], x_tab[:].bitcast(U32).indirect(offs_t[:]))
 
         w_bf = sbuf([P, PACK, P, PACK], BF16, "w_bf")
@@ -119,7 +123,11 @@ def tile_picked_ydrlogi_ev_p_kernel(
 
         nc.vector.tensor_copy(e_codes[:], e_tab[:].bitcast(U32).indirect(voc_t[:]))
 
-        share = [sbuf([P, S], F32, "share%d" % t, tag="e_tab_then_y1" if t == 1 else None) for t in range(PACK)]
+        slot_bytes = 4 * S
+        share = [
+            placed([P, S], F32, "share%d" % t, t // 2 * slot_bytes) if t % 2 else sbuf([P, S], F32, "share%d" % t)
+            for t in range(PACK)
+        ]
         for t in range(0, PACK, 2):
             nc.scalar.activation(share[t][:], y_ps[t][:], ACT.Copy, scale=PARENT_SHARE)
             nc.vector.tensor_scalar(share[t + 1][:], y_ps[t + 1][:], PARENT_SHARE, None, ALU.mult)
@@ -205,7 +213,7 @@ def tile_picked_ydrlogi_ev_p_kernel(
         for u in range(2):
             nc.scalar.activation(parent[:, u, :], share[2 + u][:].indirect(par_t[:, entries(1)]), ACT.Copy)
 
-        bias_gained = sbuf([P, Z], F32, "bias_gained", tag="share3")
+        bias_gained = placed([P, Z], F32, "bias_gained", slot_bytes)
         nc.scalar.activation(bias_gained[:], bias_tab[:].indirect(voc_t[:]), ACT.Copy, scale=OUT_GAIN)
 
         hid0 = sbuf([P, P * PACK], BF16, "hid0", tag="hid0_then_nd1")

from contextlib import ExitStack

import concourse.mybir as mybir

F32 = mybir.dt.float32
BF16 = mybir.dt.bfloat16
I32 = mybir.dt.int32
U32 = mybir.dt.uint32
U16 = mybir.dt.uint16
U8 = mybir.dt.uint8
FP8X4 = mybir.dt.float8_e4m3fn_x4
ACT = mybir.ActivationFunctionType
ALU = mybir.AluOpType

P = 128
PACK = 4
BLOCKS = 16
QUAD = 32
GROUP = 16
RUN = 4
K, T, S, H, V, Z, W = 512, 2048, 512, 512, 256, 512, 2048
FLOPS = 2 * K * H * S + 2 * H * V * Z

PARENT_SHARE = 0.6
CAP_GAIN = 1.3
OUT_GAIN = 100.0
W_SPLIT = 84


def tile_picked_ydrlogi_ev_p_kernel(
    tc, x_words, x_scales, w1, e_words, e_scales, unit, bias, offs, node, par, voc, out
):
    nc = tc.nc
    halves = range(V // P)
    parts = [slice(0, Z // 2), slice(Z // 2, Z)]

    with ExitStack() as ctx:
        keep = ctx.enter_context(tc.tile_pool(name="keep", bufs=1))
        reuse = ctx.enter_context(tc.tile_pool(name="reuse", bufs=1))
        psum = ctx.enter_context(tc.psum_pool(name="psum", bufs=1))

        def sbuf(shape, dtype, name, tag=None):
            return keep.tile(shape, dtype, name=name, tag=tag or name, align_bytes=64)

        def placed(shape, dtype, name, offset):
            return reuse.tile(shape, dtype, name=name, offset=offset, align_bytes=64)

        offs_t = sbuf([P, S // GROUP], U16, "offs_t")
        node_t = sbuf([P, V // GROUP], U16, "node_t")
        par_t = sbuf([P, V // GROUP], U16, "par_t")
        voc_t = sbuf([P, Z // GROUP], U16, "voc_t")
        x_tab = sbuf([P, T], I32, "x_tab")
        xs_tab = sbuf([P, T], U8, "xs_tab")
        es_tab = placed([P, W], U8, "es_tab", 0)
        w_raw = sbuf([P, PACK, H], F32, "w_raw", tag="w_raw_then_bias")
        unit_t = sbuf([P, PACK], F32, "unit_t")
        x_codes = sbuf([P, S], U32, "x_codes")
        x_rows = sbuf([P, S], U8, "x_rows")
        x_plane = sbuf([P, S], U8, "x_plane")
        e_codes = sbuf([P, Z], U32, "e_codes")
        e_rows = sbuf([P, Z], U8, "e_rows")
        e_plane = sbuf([P, Z], U8, "e_plane")

        for engine, tab, plane in ((nc.vector, xs_tab, x_plane), (nc.gpsimd, es_tab, e_plane)):
            engine.memset(tab[QUAD : 2 * QUAD, :].bitcast(I32), 0)
            engine.memset(tab[2 * QUAD : P, :].bitcast(I32), 0)
            engine.memset(plane[:].bitcast(I32), 0)

        def load_scales(tab, scales):
            rows = scales[0].bitcast(I32)
            twice = rows.unsqueeze(1).to_broadcast([BLOCKS, 2, rows.shape[1]])
            nc.sync.dma_start(out=tab[0:QUAD, :].bitcast(I32), in_=twice)

        def place_scales(plane, rows):
            for r in range(4):
                nc.sync.dma_start(out=plane[r:P:QUAD, :].bitcast(I32), in_=rows[2 * r : QUAD : 8, :].bitcast(I32))

        nc.sync.dma_start(offs_t[:], offs)
        load_scales(xs_tab, x_scales)
        nc.sync.dma_start(voc_t[:], voc)
        load_scales(es_tab, e_scales)
        nc.sync.dma_start(out=unit_t[:], in_=unit.rearrange("(p t) o -> p (t o)", t=PACK))
        nc.sync.dma_start(out=x_tab[:], in_=x_words[0].rearrange("p n t -> p (n t)").bitcast(I32))
        nc.sync.dma_start(out=w_raw[:], in_=w1.rearrange("(p j) c -> p j c", j=PACK))
        nc.sync.dma_start(node_t[:], node)
        nc.sync.dma_start(par_t[:], par)

        nc.vector.tensor_copy(x_rows[:], xs_tab[:].indirect(offs_t[:]))
        place_scales(x_plane, x_rows)
        nc.vector.tensor_copy(e_rows[:], es_tab[:].indirect(voc_t[:]))
        e_tab = placed([P, W], I32, "e_tab", 0)
        nc.sync.dma_start(out=e_tab[:], in_=e_words[0].rearrange("p n t -> p (n t)").bitcast(I32))
        place_scales(e_plane, e_rows)
        nc.vector.tensor_copy(x_codes[:], x_tab[:].bitcast(U32).indirect(offs_t[:]))

        w_bf = sbuf([P, PACK, P, PACK], BF16, "w_bf")
        w_dst = w_bf[:].rearrange("p t m j -> p m t j")
        w_src = w_raw[:].rearrange("p j (m t) -> p m t j", t=PACK)
        nc.vector.tensor_copy(out=w_dst[:, 0:W_SPLIT], in_=w_src[:, 0:W_SPLIT])
        nc.scalar.copy(out=w_dst[:, W_SPLIT:P], in_=w_src[:, W_SPLIT:P])

        y_ps = []
        for t in range(PACK):
            w_codes = sbuf([P, P], U32, "w_codes%d" % t)
            w_plane = sbuf([P, P], U8, "w_plane%d" % t)
            nc.vector.quantize_mx(
                out=w_codes[:].bitcast(FP8X4), scales=w_plane[:], in_=w_bf[:, t].rearrange("p m j -> p (m j)")
            )
            y_slot = psum.tile([P, S], F32, name="y_ps%d" % t)
            nc.tensor.matmul_mx(
                out=y_slot[:],
                lhsT=w_codes[:].bitcast(FP8X4),
                lhsT_scale=w_plane[:],
                rhs=x_codes[:].bitcast(FP8X4),
                rhs_scale=x_plane[:],
                start=True,
                stop=True,
            )
            y_ps.append(y_slot)

        bias_tab = sbuf([P, W], F32, "bias_tab", tag="w_raw_then_bias")
        nc.sync.dma_start(out=bias_tab[:], in_=bias)

        nc.vector.tensor_copy(e_codes[:], e_tab[:].bitcast(U32).indirect(voc_t[:]))

        slot_bytes = 4 * S
        share = [
            placed([P, S], F32, "share%d" % t, t // 2 * slot_bytes) if t % 2 else sbuf([P, S], F32, "share%d" % t)
            for t in range(PACK)
        ]
        for t in range(0, PACK, 2):
            nc.scalar.activation(share[t][:], y_ps[t][:], ACT.Copy, scale=PARENT_SHARE)
            nc.vector.tensor_scalar(share[t + 1][:], y_ps[t + 1][:], PARENT_SHARE, None, ALU.mult)

        def entries(h):
            return slice(h * P // GROUP, (h + 1) * P // GROUP)

        own = {}
        bounded = [sbuf([P, PACK, P], F32, "bounded%d" % h) for h in halves]
        for h in halves:
            own[h] = sbuf([P, PACK, P], F32, "own%d" % h, tag="own")
            for t0 in range(0, PACK, 2):
                for t in (t0, t0 + 1):
                    picked = share[t][:].indirect(node_t[:, entries(h)])
                    if (h, t) == (0, PACK - 1):
                        nc.vector.tensor_copy(own[h][:, t, :], picked)
                    else:
                        nc.scalar.activation(own[h][:, t, :], picked, ACT.Copy)
                pair = slice(t0, t0 + 2)
                nc.scalar.activation(bounded[h][:, pair, :], own[h][:, pair, :], ACT.Tanh, scale=1.0 / PARENT_SHARE)

        def add_parent(nd, h, t):
            nc.vector.tensor_tensor(
                nd[:, t, :], share[t][:].indirect(par_t[:, entries(h)]), bounded[h][:, t, :], ALU.add
            )

        def make_hid(hid, nd):
            nc.vector.tensor_tensor(
                hid[:].rearrange("p (c i t) -> p c t i", i=RUN, t=PACK),
                nd[:].rearrange("p t (c i) -> p c t i", i=RUN),
                unit_t[:].unsqueeze(1).unsqueeze(3).to_broadcast([P, P // RUN, PACK, RUN]),
                ALU.mult,
            )

        sc_ps = {}

        def score(hid, h):
            h_codes = sbuf([P, P], U32, "h_codes%d" % h)
            h_plane = sbuf([P, P], U8, "h_plane%d" % h)
            nc.vector.quantize_mx(out=h_codes[:].bitcast(FP8X4), scales=h_plane[:], in_=hid[:])
            for c, cols in enumerate(parts):
                sc_ps[h, c] = psum.tile([P, Z // 2], F32, name="sc_ps%d_%d" % (h, c))
                nc.tensor.matmul_mx(
                    out=sc_ps[h, c][:],
                    lhsT=h_codes[:].bitcast(FP8X4),
                    lhsT_scale=h_plane[:],
                    rhs=e_codes[:, cols].bitcast(FP8X4),
                    rhs_scale=e_plane[:, cols],
                    start=True,
                    stop=True,
                )

        gained = [sbuf([P, Z], F32, "gained%d" % h) for h in halves]
        capped = [sbuf([P, Z], F32, "capped%d" % h) for h in halves]
        el = [sbuf([P, Z], F32, "el%d" % h) for h in halves]
        tot = [sbuf([P, 1], F32, "tot%d" % h) for h in halves]

        def cap(h, c):
            cols = parts[c]
            nc.vector.scalar_tensor_tensor(
                gained[h][:, cols], sc_ps[h, c][:], OUT_GAIN, bias_gained[:, cols], ALU.mult, ALU.add
            )
            nc.scalar.activation(capped[h][:, cols], gained[h][:, cols], ACT.Tanh, scale=1.0 / OUT_GAIN)

        def weigh(h):
            nc.scalar.activation(el[h][:], capped[h][:], ACT.Exp, scale=CAP_GAIN, accum_out=tot[h][:])

        def finish(h):
            inv = sbuf([P, 1], F32, "inv%d" % h)
            res = sbuf([P, Z], F32, "res%d" % h)
            nc.vector.reciprocal(inv[:], tot[h][:])
            for cols in parts:
                nc.vector.scalar_tensor_tensor(
                    res[:, cols], el[h][:, cols], inv[:], gained[h][:, cols], ALU.mult, ALU.mult
                )
                nc.sync.dma_start(out=out[h * P : (h + 1) * P, cols], in_=res[:, cols])

        nd0 = sbuf([P, PACK, P], F32, "nd0")
        for t in range(PACK):
            add_parent(nd0, 0, t)

        parent = own[1][:, 0:2, :]
        for u in range(2):
            nc.scalar.activation(parent[:, u, :], share[2 + u][:].indirect(par_t[:, entries(1)]), ACT.Copy)

        bias_gained = placed([P, Z], F32, "bias_gained", slot_bytes)
        nc.scalar.activation(bias_gained[:], bias_tab[:].indirect(voc_t[:]), ACT.Copy, scale=OUT_GAIN)

        hid0 = sbuf([P, P * PACK], BF16, "hid0", tag="hid0_then_nd1")
        make_hid(hid0, nd0)
        score(hid0, 0)

        nd1 = sbuf([P, PACK, P], F32, "nd1", tag="hid0_then_nd1")
        for t in range(2):
            add_parent(nd1, 1, t)
        nc.vector.tensor_tensor(nd1[:, 2:PACK, :], parent, bounded[1][:, 2:PACK, :], ALU.add)
        hid1 = sbuf([P, P * PACK], BF16, "hid1")
        make_hid(hid1, nd1)
        cap(0, 0)
        score(hid1, 1)
        cap(0, 1)
        weigh(0)
        cap(1, 0)
        cap(1, 1)
        weigh(1)
        for h in halves:
            finish(h)
